import numpy as np
CORES = [5,21,45,77,85,101,109,125,133,141,189,213]
N = 12
T, SQ = 4096, 2048
def entries(a): return a.T.reshape(-1)
def pack(v, P): return np.ascontiguousarray(np.asarray(v, np.int32).reshape(-1, P).T)
def lists(rng, how):
    d = np.concatenate([[0], rng.integers(1 - SQ // 2, SQ // 2, N - 1), [int(rng.integers(1 - SQ // 2, 1))]])
    if how == "lag": d[1:] = -SQ
    if how == "lead": d[1:N] = SQ; d[N] = 0
    if how == "runs": m = int(rng.integers(1, N - 2)); d[m] = -abs(d[m]); d[m + 1] = d[m] + SQ; d[m + 2] = d[m]
    if how == "skew": t = int(rng.integers(2, N - 1)); d[1:] = rng.integers(SQ // 2 + 1, SQ - 1, N); d[t + 1:] *= -1; d[t] = d[t - 1] + d[t + 1]
    n = SQ + np.diff(d)
    F = np.zeros((N, T), np.int64)
    for r in range(N):
        o = rng.permutation(T)
        if how == "runs": o = (T // 16 * rng.permutation(16)[:, None] + np.arange(T // 16)).reshape(-1)
        if how == "skew": o = np.concatenate([[0, T - 1], 1 + rng.permutation(T - 2)])
        F[r, o[:n[r]]] = 1
    return {"fl": np.stack([pack(f, 16) for f in F])}
def setup_inputs(rng):
    return dict({"x": rng.standard_normal((N, 128, T), dtype=np.float32), "st": rng.standard_normal((N, 128, SQ), dtype=np.float32)}, **lists(rng, "uniform"))
def setup_inputs_lag(rng):
    d = setup_inputs(rng); d.update(lists(rng, "lag"))
    for k in ("x", "st"): d[k] = (d[k].astype(np.float32) * 1048576.0).astype(d[k].dtype)
    return d
def setup_inputs_lead(rng):
    d = setup_inputs(rng); d.update(lists(rng, "lead"))
    for k in ("x", "st"): d[k] = (d[k].astype(np.float32) * (1 / 1024.0)).astype(d[k].dtype)
    return d
def setup_inputs_runs(rng):
    d = setup_inputs(rng); d.update(lists(rng, "runs"))
    return d
def setup_inputs_skew(rng):
    d = setup_inputs(rng); d.update(lists(rng, "skew"))
    return d
def check_inputs(x):
    bad = []
    if x["fl"].min() < 0 or x["fl"].max() >= 2: bad.append("fl out of range")
    if int(x["fl"].sum()) > N * SQ: bad.append("more flags than the stream has columns")
    c = np.concatenate([[0], np.cumsum([int(a.sum()) for a in x["fl"]])])
    if any(c[r] < (r - 1) * SQ or c[r + 1] > (r + 2) * SQ for r in range(N)): bad.append("a rank's share of the stream reaches beyond its neighbours' parts")
    return bad
def reference(x, st, fl):
    S = np.concatenate(list(st), axis=1); X = np.concatenate(list(x), axis=1)
    F = np.concatenate([entries(f) for f in fl]) > 0; c = np.cumsum(F) - F
    Y = np.where(F[None, :], S[:, np.minimum(c, N * SQ - 1)], X)
    return {"y": np.stack([Y[:, T * r:T * r + T] for r in range(N)])}

from concourse.bass import DstId, RemoteDMATransfer
from concourse.mybir import dt, AluOpType, AxisListType, ActivationFunctionType

N = 12
TC, SQ = 4096, 2048
WORLD = 256
PREV, OWN, NEXT, WEND = TC, TC + SQ, TC + 2 * SQ, TC + 3 * SQ
FW = 32
Q = SQ // 4
X0 = 1024
BLOCKS = [384, 384, 768, 768, 896, 896]

SCRATCH = {
    "win": ("sbuf", [128, WEND], "float32"),
    "yb": ("sbuf", [128, TC], "float32"),
    "hb": ("sbuf", [128, Q], "float32"),
    "fr": ("sbuf", [128, N * FW], "int32"),
    "frb": ("sbuf", [128, N * FW], "bfloat16"),
    "fli": ("sbuf", [128, 256], "int32"),
    "flb": ("sbuf", [128, 256], "bfloat16"),
    "dd": ("sbuf", [128, 128], "float32"),
    "ju": ("sbuf", [128, 256], "float32"),
    "jj": ("sbuf", [128, 256], "float32"),
    "pi": ("sbuf", [128, 16], "int32"),
    "pm": ("sbuf", [128, 16], "int32"),
    "pf": ("sbuf", [128, 16], "float32"),
    "rep": ("sbuf", [128, 128], "bfloat16"),
    "tri": ("sbuf", [128, 128], "bfloat16"),
    "one": ("sbuf", [128, 128], "bfloat16"),
    "zer": ("sbuf", [128, 256], "float32"),
    "sc": ("sbuf", [128, 256], "float32"),
    "e1": ("sbuf", [128, 256], "float32"),
    "e2": ("sbuf", [128, 256], "float32"),
    "e3": ("sbuf", [128, 256], "float32"),
    "aa": ("sbuf", [128, 256], "float32"),
    "t1": ("sbuf", [128, 256], "float32"),
    "t2": ("sbuf", [128, 256], "float32"),
    "base": ("sbuf", [128, 16], "float32"),
    "off": ("sbuf", [128, 256], "uint16"),
    "flc": ("dram", [128, FW], "int32"),
    "hf": ("dram", [128, FW], "int32"),
    "pa": ("psum", [128, 512], "float32"),
    "pb": ("psum", [128, 512], "float32"),
    "pc": ("psum", [128, 512], "float32"),
    "pd": ("psum", [128, 512], "float32"),
}
SEMAPHORES = ["s_st0", "s_st1", "s_fc", "s_fl", "s_x", "s_go", "s_io", "s_v", "s_t", "s_y", "left",
              "h_fl", "h_st", "a_fl", "a_st"] + ["g%d" % k for k in range(len(BLOCKS))]

_plan = {}


def chip_mates(topo, c):
    return [k for k in range(WORLD) if k != c and topo.host(k) == topo.host(c) and topo.chip(k) == topo.chip(c)]


def plan(T, topo):
    if _plan:
        return _plan
    for r, c in enumerate(T.cores):
        near = chip_mates(topo, c)
        own = [k for k in near if any(topo.mates(k, m) and topo.may_write(k, m) for m in range(WORLD))]
        own.sort(key=lambda k: (topo.die(k) == topo.die(c), k))
        rest = [k for k in near if k not in own]
        serve = {k: [] for k in own + rest}
        higher = list(T.cores[r + 1:])
        cross = [d for d in higher if not topo.may_write(c, d)]
        same = [d for d in higher if topo.may_write(c, d)]
        for d in cross:
            k = min(own, key=lambda h: len(serve[h]))
            serve[k].append(d)
        for d in same:
            k = min(own + rest, key=lambda h: len(serve[h]))
            serve[k].append(d)
        _plan[r] = {"core": c, "own": own, "serve": {k: v for k, v in serve.items() if v}}
    return _plan


def engines(mask, parts):
    bits = [1 << i for i in range(mask.bit_length()) if mask >> i & 1]
    n = len(bits) // parts
    return [sum(bits[i * n:(i + 1) * n]) for i in range(parts)]


def to(topo, d, src):
    rid, pid = topo.addr(d, src)
    return DstId(rid=rid, pnc=pid)


def rank_program(g, core, T, topo):
    P = plan(T, topo)
    rank = T.rank_of(core)
    if rank is not None:
        return run_rank(g, core, rank, T, topo, P)
    for r in range(N):
        if core in P[r]["own"] or core in P[r]["serve"]:
            return run_helper(g, core, r, T, topo, P)


def run_helper(g, core, r, T, topo, P):
    sem = T.sem
    left = 0
    full = bin(topo.mask(T.cores[r], core)).count("1")
    ds = P[r]["serve"].get(core, [])
    if ds:
        m = topo.mask(core, ds[0])
        g.wait_ge(sem.h_fl, full)
        g.remote_dma_fused([RemoteDMATransfer(dst_ids=[to(topo, d, core) for d in ds], dma_engine_mask=m, remote_sem=sem.a_fl,
                                              srcs=[T.hf[:]], dsts=[T.fr[:, r * FW:(r + 1) * FW] for d in ds])],
                           local_sem=sem.left)
        left += bin(m).count("1")
    if core in P[r]["own"]:
        q = P[r]["own"].index(core)
        ids, dsts, m = [], [], 0
        for n, at in ((r - 1, NEXT), (r + 1, PREV)):
            if 0 <= n < N:
                ids.append(to(topo, T.cores[n], core))
                dsts.append(T.win[:, at + q * Q:at + (q + 1) * Q])
                m = topo.mask(core, T.cores[n])
        g.wait_ge(sem.h_st, full // 2)
        g.remote_dma_fused([RemoteDMATransfer(dst_ids=ids, dma_engine_mask=m, remote_sem=sem.a_st, srcs=[T.hb[:]], dsts=dsts)],
                           local_sem=sem.left)
        left += bin(m).count("1")
    g.wait_ge(sem.left, left)


def run_rank(g, core, r, T, topo, P):
    sem = T.sem
    own, serve = P[r]["own"], P[r]["serve"]
    nports = bin(topo.mask(own[0], T.cores[r - 1 if r else 1])).count("1")
    xo = SQ if r == 0 else 0
    wend = NEXT if r == N - 1 else WEND
    half = SQ // 2

    g.sync.dma_start(T.win[:, OWN:OWN + half], T.st[:, 0:half]).then_inc(sem.s_st0, 16)
    if serve:
        g.scalar.dma_start(T.flc[:], T.fl[:]).then_inc(sem.s_fc, 16)
    g.scalar.dma_start(T.fli[0:16, :], T.fl[:]).then_inc(sem.s_fl, 16)
    g.sync.dma_start(T.win[:, OWN + half:OWN + SQ], T.st[:, half:SQ]).then_inc(sem.s_st1, 16)
    g.sync.dma_start(T.win[:, xo:xo + X0], T.x[:, 0:X0]).then_inc(sem.s_x, 16)
    g.sync.wait_ge(sem.s_go, 1)
    g.sync.dma_start(T.win[:, xo + X0:xo + TC], T.x[:, X0:TC]).then_inc(sem.s_x, 16)

    g.iota(T.dd[0:16, :], [[0, 8], [1, 16]], 0, -1, allow_small_or_imprecise_dtypes=True).then_inc(sem.s_io, 1)
    g.iota(T.pi[:, 0:1], [[0, 1]], 0, 1).then_inc(sem.s_io, 1)
    g.iota(T.ju[:], [[16, 256]], 0, 0, allow_small_or_imprecise_dtypes=True).then_inc(sem.s_io, 1)
    left = 0
    if serve:
        hs = list(serve)
        m = topo.mask(core, hs[0])
        g.wait_ge(sem.s_fc, 16)
        g.remote_dma_fused([RemoteDMATransfer(dst_ids=[to(topo, h, core) for h in hs], dma_engine_mask=m, remote_sem=sem.h_fl,
                                              srcs=[T.flc[:]], dsts=[T.hf[:] for h in hs])], local_sem=sem.left)
        left += bin(m).count("1")
    for k, s in ((0, sem.s_st0), (1, sem.s_st1)):
        g.wait_ge(s, 16)
        tr = []
        for i in (0, 1):
            q = 2 * k + i
            h = own[q]
            m = engines(topo.mask(core, h), 2)[i]
            tr.append(RemoteDMATransfer(dst_ids=[to(topo, h, core)], dma_engine_mask=m, remote_sem=sem.h_st,
                                        srcs=[T.win[:, OWN + q * Q:OWN + (q + 1) * Q]], dsts=[T.hb[:]]))
            left += bin(m).count("1")
        g.remote_dma_fused(tr, local_sem=sem.left)
    g.sem_inc(sem.s_go, 1)
    g.wait_ge(sem.left, left)

    nv, nt = [0], [0]

    def vec(f, *a):
        if nv[0]:
            g.vector.wait_ge(sem.s_v, nv[0])
        f(*a).then_inc(sem.s_v, 1)
        nv[0] += 1

    def mm(out, a, b):
        g.tensor.matmul(out, a, b, start=True, stop=True).then_inc(sem.s_t, 1)
        nt[0] += 1

    A, v = AluOpType, g.vector
    vec(v.memset, T.one[:], 1.0)
    vec(v.memset, T.zer[:], 0.0)
    v.wait_ge(sem.s_io, 3)
    vec(v.tensor_scalar, T.rep[0:16, :], T.dd[0:16, :], 0.0, None, A.is_equal)
    vec(v.tensor_scalar, T.tri[0:16, :], T.dd[0:16, :], 0.0, 1.0, A.is_gt, A.subtract)
    vec(v.tensor_scalar, T.pm[:, 0:1], T.pi[:, 0:1], 15, None, A.bitwise_and)
    vec(v.tensor_copy, T.pf[:, 0:1], T.pm[:, 0:1])
    vec(v.tensor_scalar, T.jj[:], T.ju[:], T.pf[:, 0:1], None, A.add)
    v.wait_ge(sem.s_fl, 16)
    vec(v.tensor_copy, T.flb[0:16, :], T.fli[0:16, :])
    g.tensor.wait_ge(sem.s_v, nv[0])
    mm(T.pb[:, 0:256], T.one[0:16, :], T.flb[0:16, :])
    mm(T.pa[:, 0:256], T.tri[0:16, :], T.flb[0:16, :])
    mm(T.pc[:, 0:256], T.rep[0:16, :], T.flb[0:16, :])
    v.wait_ge(sem.s_t, nt[0])
    vec(v.tensor_tensor_scan, T.sc[:], T.pb[:, 0:256], T.zer[:], float(OWN - xo - SQ * r), A.add, A.add)
    vec(v.tensor_tensor, T.e1[:], T.sc[:], T.pa[:, 0:256], A.add)
    vec(v.tensor_tensor, T.e2[:], T.e1[:], T.jj[:], A.subtract)
    vec(v.tensor_tensor, T.e3[:], T.e2[:], T.pc[:, 0:256], A.mult)
    vec(v.tensor_tensor, T.aa[:], T.e3[:], T.jj[:], A.add)
    lst = T.aa
    if r:
        w = r * FW
        v.wait_ge(sem.a_fl, r * nports)
        vec(v.tensor_copy, T.frb[:, 0:w], T.fr[:, 0:w])
        g.tensor.wait_ge(sem.s_v, nv[0])
        mm(T.pd[:, 0:w], T.one[:], T.frb[:, 0:w])
        v.wait_ge(sem.s_t, nt[0])
        vec(v.tensor_reduce, T.base[:, 0:1], T.pd[:, 0:w], AxisListType.X, A.add)
        vec(v.tensor_scalar, T.t1[:], T.pc[:, 0:256], T.base[:, 0:1], None, A.mult)
        vec(v.tensor_tensor, T.t2[:], T.t1[:], T.aa[:], A.add)
        lst = T.t2
    vec(v.tensor_copy, T.off[:], lst[:])

    parts = (1 if r else 0) + (1 if r < N - 1 else 0)
    for e in (g.vector, g.scalar):
        e.wait_ge(sem.s_v, nv[0])
        e.wait_ge(sem.s_st0, 16)
        e.wait_ge(sem.s_st1, 16)
        e.wait_ge(sem.s_x, 32)
        e.wait_ge(sem.a_st, parts * len(own) * nports)
    a = 0
    for k, n in enumerate(BLOCKS):
        src = T.win[:, xo:wend].indirect(T.off[:, a // 16:(a + n) // 16])
        out = T.yb[:, a:a + n]
        s = T.sem["g%d" % k]
        if k % 2 == 0:
            g.vector.tensor_copy(out, src).then_inc(s, 1)
        else:
            g.scalar.activation(out, src, ActivationFunctionType.Copy).then_inc(s, 1)
        g.sync.wait_ge(s, 1)
        g.sync.dma_start(T.y[:, a:a + n], out).then_inc(sem.s_y, 16)
        a += n
    g.sync.wait_ge(sem.s_y, 16 * len(BLOCKS))
